import numpy as np
import ml_dtypes


def mxq(x, axis, fmt="e4m3"):
    dtype, down = {"e4m3": (ml_dtypes.float8_e4m3fn, 7), "e5m2": (ml_dtypes.float8_e5m2, 14)}[fmt]
    v = np.moveaxis(np.asarray(x, np.float32).astype(ml_dtypes.bfloat16).astype(np.float64), axis, -1)
    blocks = v.reshape(v.shape[:-1] + (-1, 32))
    amax = np.abs(blocks).max(-1, keepdims=True)
    byte = np.maximum(np.where(amax > 0, np.frexp(amax)[1] - 1 + 127, 0) - down, 1)
    scale = np.exp2(byte - 127.0)
    codes = (blocks / scale).astype(np.float32).astype(dtype).astype(np.float64)
    return np.moveaxis((codes * scale).reshape(v.shape), -1, axis)


WIDE = False


def mx_kscale(k):
    if not WIDE:
        return np.ones(k)
    levels = np.array([10, -10, 5, -5, 0])
    if k % 512:
        return np.exp2(np.random.permutation(np.resize(levels, k // 32))).repeat(32)
    a = np.empty((k // 512, 16))
    for p in range(k // 512):
        a[p, :8] = np.random.permutation(np.resize(levels, 8))
        for g in range(8):
            far = levels[np.abs(levels - a[p, g]) >= 10]
            a[p, g + 8] = far[np.random.randint(len(far))]
    return np.exp2(a.ravel()).repeat(32)


def f64(x):
    return np.asarray(x).astype(np.float64)


def striped(idx):
    return np.tile(idx.reshape(-1, 16).T, (8, 1)).astype(np.uint16)


def unstriped(offs):
    return offs[:16].T.reshape(-1).astype(np.int64)


def pack_weight(w):
    k, n = w.shape
    w = f64(np.asarray(w, np.float32).astype(ml_dtypes.bfloat16)).reshape(k // 32, 32, n)
    amax = np.abs(w).max(1)
    byte = np.clip(np.where(amax > 0, np.frexp(amax)[1] - 1 + 127 - 7, 1), 1, 254)
    scaled = (w * np.exp2(127.0 - byte)[:, None, :]).reshape(k, n).astype(np.float32)
    words = np.ascontiguousarray(scaled.reshape(k // 512, 128, 4, n).transpose(0, 1, 3, 2)).astype(ml_dtypes.float8_e4m3fn).view(np.uint8)
    return words, np.ascontiguousarray(byte.astype(np.uint8).reshape(k // 512, 16, n))


def unpack_weight(words, scales):
    g, p, n, _ = words.shape
    vals = np.ascontiguousarray(words).view(ml_dtypes.float8_e4m3fn).astype(np.float64) * np.repeat(np.exp2(scales.astype(np.float64) - 127.0), 8, axis=1)[..., None]
    return vals.transpose(0, 1, 3, 2).reshape(g * 512, n)

def planes(y):
    n, m = y.shape
    v = y.astype(np.float32).astype(ml_dtypes.bfloat16).astype(np.float64).reshape(n // 32, 32, m)
    top = np.abs(v).max(1)
    byte = np.clip(np.where(top > 0, np.frexp(top)[1] - 1 + 127 - 7, 1), 1, 254)
    codes = (v * np.exp2(127.0 - byte)[:, None, :]).reshape(n, m).astype(np.float32).astype(ml_dtypes.float8_e4m3fn).view(np.uint8)
    words = codes.reshape(n // 512, 128, 4, m).transpose(0, 1, 3, 2)
    return np.ascontiguousarray(words), np.ascontiguousarray(byte.astype(np.uint8).reshape(n // 512, 16, m))


K, T, S, H, J, C = 512, 2048, 512, 512, 512, 512


def setup_inputs():
    n = np.random.standard_normal
    s = mx_kscale(K)[:, None]
    packed_xT = pack_weight(n((K, T)) * s)
    packed_w1 = pack_weight(n((K, H)) / np.sqrt(K) / s)
    return {
        "x_words": packed_xT[0],
        "x_scales": packed_xT[1],
        "w1_words": packed_w1[0],
        "w1_scales": packed_w1[1],
        "tab": n((H, J)).astype(np.float32),
        "gs": (np.random.uniform(0.5, 1.5, (K, 1)) / s).astype(np.float32),
        "wb": (n((K, S)) / np.sqrt(K) / s).astype(np.float32),
        "tau": np.random.uniform(0.3, 0.9, (C, 1)).astype(np.float32),
        "offs": striped(np.random.permutation(T)[:S]),
        "n1": striped(np.random.randint(0, J, S)),
        "n2": striped(np.random.permutation(S)),
        "cand": striped(np.random.permutation(T)[:C]),
        "cb": striped(np.random.permutation(T)[:C]),
        "n3": striped(np.random.permutation(S)),
        "n4": striped(np.random.permutation(S)),
    }


def reference(x_words, x_scales, w1_words, w1_scales, tab, gs, wb, tau, offs, n1, n2, cand, cb, n3, n4):
    x_cb = unpack_weight(x_words, x_scales)[:, unstriped(cb)]
    b = x_cb.T @ mxq(f64(wb), 0, "e4m3")
    top = b.max(axis=1, keepdims=True)
    ea = np.exp(f64(tau) * (b[:, unstriped(n3)] - top))
    x_cand = unpack_weight(x_words, x_scales)[:, unstriped(cand)]
    xq = unpack_weight(x_words, x_scales)[:, unstriped(offs)]
    y = unpack_weight(w1_words, w1_scales).T @ xq
    z = f64(gs) * (np.maximum(y + f64(tab)[:, unstriped(n1)], y[:, unstriped(n2)]))
    a = 0.0625 * ((x_cand.T @ mxq(z, 0, "e4m3")))
    out_0 = (2.0 * ea) * (a - a[:, unstriped(n4)]) - (0.5 * b)
    return (out_0,) + planes(out_0)

@@ -1,0 +1,232 @@
+from contextlib import ExitStack
+
+import concourse.mybir as mybir
+
+K, T, S, H, J, C = 512, 2048, 512, 512, 512, 512
+FLOPS = 2 * K * C * S + 2 * K * H * S + 2 * H * C * S
+
+F32 = mybir.dt.float32
+BF16 = mybir.dt.bfloat16
+I32 = mybir.dt.int32
+U32 = mybir.dt.uint32
+U16 = mybir.dt.uint16
+U8 = mybir.dt.uint8
+FP8X4 = mybir.dt.float8_e4m3fn_x4
+ALU = mybir.AluOpType
+ACT = mybir.ActivationFunctionType
+
+P = 128
+PACK = 4
+SPARE = 16
+
+
+def tile_picked_cdswpxbkind_none_po_kernel(
+    tc, x_words, x_scales, w1_words, w1_scales, tab, gs, wb, tau, offs, n1, n2, cand, cb, n3, n4, out_0, out_1, out_2
+):
+    nc = tc.nc
+    with ExitStack() as ctx:
+        keep = ctx.enter_context(tc.tile_pool(name="keep", bufs=1))
+        psum = ctx.enter_context(tc.psum_pool(name="psum", bufs=1))
+
+        def sb(name, shape, dtype):
+            return keep.tile(shape, dtype, name=name, align_bytes=64)
+
+        def load_list(name, src):
+            tile = sb(name, [P, S // 16], U16)
+            nc.sync.dma_start(tile[:], src)
+            return tile
+
+        def load_scale_rows_spread(queue, tile, src):
+            for q in range(4):
+                rows = src[0, 4 * q : 4 * q + 4, :].bitcast(I32)
+                queue.dma_start(tile[32 * q : 32 * q + 32, :].bitcast(I32), rows.partition_broadcast(8))
+
+        def dealt(tile):
+            return tile[:].rearrange("p (t m) -> p m t", t=PACK)
+
+        def interleave(copy, dst, src):
+            copy(
+                dst[:].rearrange("p (c i) t -> p c t i", i=4),
+                src[:].rearrange("p t (c i) -> p c t i", i=4),
+            )
+
+        xw = sb("xw", [P, T], U32)
+        xs = sb("xs", [P, T], U8)
+        w1w_raw = sb("w1w_raw", [P, H], U32)
+        w1s_raw = sb("w1s_raw", [P, H], U8)
+        tab_win = [sb("tab_win%d" % t, [P, J + SPARE], F32) for t in range(PACK)]
+        y_win = [sb("y_win%d" % t, [P, S + SPARE], F32) for t in range(PACK)]
+        a_win = [sb("a_win%d" % t, [P, S + SPARE], F32) for t in range(PACK)]
+        b_win = [sb("b_win%d" % t, [P, 2 * S], F32) for t in range(PACK)]
+        wb_raw = sb("wb_raw", [P, PACK, S], F32)
+        gs_sb = sb("gs_sb", [P, PACK], F32)
+        tau_sb = sb("tau_sb", [P, PACK], F32)
+        wb_codes = sb("wb_codes", [P, S], U32)
+        wb_scale = sb("wb_scale", [P, S], U8)
+        z_codes = sb("z_codes", [P, S], U32)
+        z_scale = sb("z_scale", [P, S], U8)
+
+        nc.vector.memset(wb_scale[:].bitcast(I32), 0)
+        nc.vector.memset(z_scale[:].bitcast(I32), 0)
+        for t in range(PACK):
+            nc.vector.memset(tab_win[t][:, J:], 0.0)
+        for t in range(PACK):
+            nc.vector.memset(y_win[t][:, S:], 0.0)
+
+        offs_sb = load_list("offs_sb", offs)
+        load_scale_rows_spread(nc.scalar, xs, x_scales)
+        cb_sb = load_list("cb_sb", cb)
+        cand_sb = load_list("cand_sb", cand)
+        nc.sync.dma_start(xw[:].bitcast(I32), x_words[0].rearrange("p n t -> p (n t)").bitcast(I32))
+        n1_sb = load_list("n1_sb", n1)
+        tab_rows = tab.rearrange("(p t) j -> p t j", t=PACK)
+        nc.sync.dma_start(tab_win[0][:, :J], tab_rows[:, 0, :])
+        nc.sync.dma_start(w1w_raw[:].bitcast(I32), w1_words[0].rearrange("p n t -> p (n t)").bitcast(I32))
+        load_scale_rows_spread(nc.sync, w1s_raw, w1_scales)
+        nc.gpsimd.dma_start(gs_sb[:], gs.rearrange("(p t) o -> p (t o)", t=PACK))
+        nc.gpsimd.dma_start(tau_sb[:], tau.rearrange("(p t) o -> p (t o)", t=PACK))
+        nc.sync.dma_start(tab_win[1][:, :J], tab_rows[:, 1, :])
+        n2_sb = load_list("n2_sb", n2)
+        nc.sync.dma_start(wb_raw[:], wb.rearrange("(p t) j -> p t j", t=PACK))
+        for t in range(2, PACK):
+            nc.sync.dma_start(tab_win[t][:, :J], tab_rows[:, t, :])
+        n3_sb = load_list("n3_sb", n3)
+        n4_sb = load_list("n4_sb", n4)
+
+        xo_w = sb("xo_w", [P, S], U32)
+        xo_s = sb("xo_s", [P, S], U8)
+        cb_w = sb("cb_w", [P, C], U32)
+        cb_s = sb("cb_s", [P, C], U8)
+        cd_w = sb("cd_w", [P, C], U32)
+        cd_s = sb("cd_s", [P, C], U8)
+        nc.vector.tensor_copy(xo_s[:], xs[:].indirect(offs_sb[:]))
+        nc.vector.tensor_copy(dealt(cb_s), xs[:].indirect(cb_sb[:]))
+        nc.vector.tensor_copy(dealt(cd_s), xs[:].indirect(cand_sb[:]))
+        nc.vector.tensor_copy(xo_w[:], xw[:].indirect(offs_sb[:]))
+        w1_s = sb("w1_s", [P, H], U8)
+        nc.vector.tensor_copy(
+            w1_s[:].rearrange("p (t m) -> p t m", t=PACK), w1s_raw[:].rearrange("p (m t) -> p t m", t=PACK)
+        )
+        nc.vector.tensor_copy(dealt(cb_w), xw[:].indirect(cb_sb[:]))
+        nc.vector.tensor_copy(dealt(cd_w), xw[:].indirect(cand_sb[:]))
+
+        w1_w = sb("w1_w", [P, H], U32)
+        tab_g = [sb("tab_g%d" % t, [P, S], F32) for t in range(PACK)]
+        nc.scalar.activation(tab_g[0][:], tab_win[0][:].indirect(n1_sb[:]), ACT.Copy)
+        nc.scalar.copy(
+            w1_w[:].rearrange("p (t m) -> p t m", t=PACK), w1w_raw[:].rearrange("p (m t) -> p t m", t=PACK)
+        )
+
+        def product(tag, lhs_w, lhs_s, rhs_w, rhs_s, t):
+            bank = psum.tile([P, S], F32, name=tag, tag=tag)
+            cols = slice(P * t, P * (t + 1))
+            nc.tensor.matmul_mx(
+                out=bank[:],
+                lhsT=lhs_w[:, cols].bitcast(FP8X4),
+                lhsT_scale=lhs_s[:, cols],
+                rhs=rhs_w[:].bitcast(FP8X4),
+                rhs_scale=rhs_s[:],
+                start=True,
+                stop=True,
+            )
+            return bank
+
+        y_ps = [product("ya%d" % t, w1_w, w1_s, xo_w, xo_s, t) for t in range(PACK)]
+
+        wb_il = sb("wb_il", [P, S, PACK], BF16)
+        interleave(nc.scalar.copy, wb_il, wb_raw)
+        for t in range(PACK):
+            nc.vector.memset(b_win[t][:, S:], 0.0)
+            nc.vector.memset(a_win[t][:, S:], 0.0)
+
+        y_g = [sb("y_g%d" % t, [P, S], F32) for t in range(PACK)]
+        u = [sb("u%d" % t, [P, S], F32) for t in range(PACK)]
+        big = [sb("big%d" % t, [P, S], F32) for t in range(PACK)]
+        z_pl = sb("z_pl", [P, PACK, S], BF16)
+        top = sb("top", [P, PACK], F32)
+        bias = sb("bias", [P, PACK], F32)
+        ea = [sb("ea%d" % t, [P, S], F32) for t in range(PACK)]
+        b_ps = []
+
+        def z_scalar(t):
+            nc.scalar.copy(y_win[t][:, :S], y_ps[t][:])
+            nc.scalar.activation(y_g[t][:], y_win[t][:].indirect(n2_sb[:]), ACT.Copy)
+            if t + 1 < PACK:
+                nc.scalar.activation(tab_g[t + 1][:], tab_win[t + 1][:].indirect(n1_sb[:]), ACT.Copy)
+
+        def z_vector(t):
+            nc.vector.tensor_tensor(u[t][:], y_ps[t][:], tab_g[t][:], ALU.add)
+            nc.vector.tensor_tensor(big[t][:], u[t][:], y_g[t][:], ALU.max)
+            nc.vector.tensor_scalar(z_pl[:, t, :], big[t][:], gs_sb[:, t : t + 1], None, ALU.mult)
+
+        def b_vector(t):
+            nc.vector.tensor_scalar(
+                b_win[t][:, :S], b_ps[t][:], 1.0, None, ALU.mult, ALU.max, accum_out=top[:, t : t + 1]
+            )
+            nc.vector.tensor_scalar(
+                bias[:, t : t + 1], top[:, t : t + 1], tau_sb[:, t : t + 1], -1.0, ALU.mult, ALU.mult
+            )
+
+        def ea_scalar(t):
+            nc.scalar.activation(
+                ea[t][:],
+                b_win[t][:].indirect(n3_sb[:]),
+                ACT.Exp,
+                bias=bias[:, t : t + 1],
+                scale=tau_sb[:, t : t + 1],
+            )
+
+        z_scalar(0)
+        z_vector(0)
+        nc.vector.quantize_mx(
+            out=wb_codes[:].bitcast(FP8X4), scales=wb_scale[:], in_=wb_il[:].rearrange("p c t -> p (c t)")
+        )
+        for t in range(PACK):
+            b_ps.append(product("b%d" % t, cb_w, cb_s, wb_codes, wb_scale, t))
+        z_scalar(1)
+        z_vector(1)
+        b_vector(0)
+        z_scalar(2)
+        b_vector(1)
+        z_vector(2)
+        z_scalar(3)
+        b_vector(2)
+        z_vector(3)
+        z_il = sb("z_il", [P, S, PACK], BF16)
+        interleave(nc.vector.tensor_copy, z_il, z_pl)
+        nc.vector.quantize_mx(
+            out=z_codes[:].bitcast(FP8X4), scales=z_scale[:], in_=z_il[:].rearrange("p c t -> p (c t)")
+        )
+        b_vector(3)
+        for t in range(PACK - 1):
+            ea_scalar(t)
+
+        a_ps = [product("ya%d" % t, cd_w, cd_s, z_codes, z_scale, t) for t in range(PACK)]
+        a_g = [sb("a_g%d" % t, [P, S], F32) for t in range(PACK)]
+        diff = [sb("diff%d" % t, [P, S], F32) for t in range(PACK)]
+        prod = [sb("prod%d" % t, [P, S], F32) for t in range(PACK)]
+        res = sb("res", [P, PACK, S], F32)
+        out_rows = out_0.rearrange("(p t) j -> p t j", t=PACK)
+        nc.vector.tensor_scalar(a_win[1][:, :S], a_ps[1][:], -0.125, None, ALU.mult)
+        for t in range(PACK):
+            if t != 1:
+                nc.scalar.activation(a_win[t][:, :S], a_ps[t][:], ACT.Copy, scale=-0.125)
+            nc.scalar.activation(a_g[t][:], a_win[t][:].indirect(n4_sb[:]), ACT.Copy)
+            nc.vector.scalar_tensor_tensor(diff[t][:], a_ps[t][:], 0.125, a_g[t][:], ALU.mult, ALU.add)
+            if t == PACK - 2:
+                ea_scalar(PACK - 1)
+            nc.vector.tensor_tensor(prod[t][:], diff[t][:], ea[t][:], ALU.mult)
+            nc.vector.scalar_tensor_tensor(res[:, t, :], b_ps[t][:], -0.5, prod[t][:], ALU.mult, ALU.add)
+            nc.sync.dma_start(out_rows[:, t, :], res[:, t, :])
+
+        o_il = sb("o_il", [P, S, PACK], BF16)
+        o_codes = sb("o_codes", [P, S], U32)
+        o_scale = sb("o_scale", [P, S], U8)
+        interleave(nc.vector.tensor_copy, o_il, res)
+        nc.vector.quantize_mx(
+            out=o_codes[:].bitcast(FP8X4), scales=o_scale[:], in_=o_il[:].rearrange("p c t -> p (c t)")
+        )
+        nc.sync.dma_start(out_1[0].rearrange("p n t -> p (n t)").bitcast(I32), o_codes[:].bitcast(I32))
+        for q in range(4):
+            queue = nc.scalar if q % 2 == 0 else nc.sync
+            queue.dma_start(out_2[0, 4 * q : 4 * q + 4, :].bitcast(I32), o_scale[32 * q : 32 * q + 4, :].bitcast(I32))

@@ -17,7 +17,14 @@ ACT = mybir.ActivationFunctionType
 
 P = 128
 PACK = 4
+LAST = PACK - 1
+LIST_ROWS = 16
 SPARE = 16
+WHOLE = slice(0, S)
+FIRST_HALF, SECOND_HALF = slice(0, S // 2), slice(S // 2, S)
+HALVES = (FIRST_HALF, SECOND_HALF)
+GAIN_ON_GPSIMD = (0, 1, 2)
+PRODUCT_ON_GPSIMD = (0, 1)
 
 
 def tile_picked_cdswpxbkind_none_po_kernel(
@@ -28,35 +35,54 @@ def tile_picked_cdswpxbkind_none_po_kernel(
         keep = ctx.enter_context(tc.tile_pool(name="keep", bufs=1))
         psum = ctx.enter_context(tc.psum_pool(name="psum", bufs=1))
 
-        def sb(name, shape, dtype):
-            return keep.tile(shape, dtype, name=name, align_bytes=64)
+        def sb(name, shape, dtype, tag=None):
+            return keep.tile(shape, dtype, name=name, tag=tag or name, align_bytes=64)
 
         def load_list(name, src):
-            tile = sb(name, [P, S // 16], U16)
+            tile = sb(name, [P, S // LIST_ROWS], U16)
             nc.sync.dma_start(tile[:], src)
             return tile
 
-        def load_scale_rows_spread(queue, tile, src):
-            for q in range(4):
-                rows = src[0, 4 * q : 4 * q + 4, :].bitcast(I32)
-                queue.dma_start(tile[32 * q : 32 * q + 32, :].bitcast(I32), rows.partition_broadcast(8))
+        def load_words(tile, src):
+            nc.sync.dma_start(tile[:].bitcast(I32), src[0].rearrange("p n t -> p (n t)").bitcast(I32))
 
         def dealt(tile):
             return tile[:].rearrange("p (t m) -> p m t", t=PACK)
 
+        def deal(copy, dst, src):
+            copy(dealt(dst), src[:].rearrange("p (m t) -> p m t", t=PACK))
+
         def interleave(copy, dst, src):
             copy(
-                dst[:].rearrange("p (c i) t -> p c t i", i=4),
-                src[:].rearrange("p t (c i) -> p c t i", i=4),
+                dst.rearrange("p (c i) t -> p c t i", i=4),
+                src.rearrange("p t (c i) -> p c t i", i=4),
             )
+
+        def quantize(codes, scale, src):
+            nc.vector.quantize_mx(out=codes.bitcast(FP8X4), scales=scale, in_=src.rearrange("p c t -> p (c t)"))
+
+        def product(tag, lhs_w, lhs_s, rhs_w, rhs_s, t, parts=(WHOLE,)):
+            bank = psum.tile([P, S], F32, name=tag, tag=tag)
+            rows = slice(P * t, P * (t + 1))
+            for cols in parts:
+                nc.tensor.matmul_mx(
+                    out=bank[:, cols],
+                    lhsT=lhs_w[:, rows].bitcast(FP8X4),
+                    lhsT_scale=lhs_s[:, rows],
+                    rhs=rhs_w[:, cols].bitcast(FP8X4),
+                    rhs_scale=rhs_s[:, cols],
+                    start=True,
+                    stop=True,
+                )
+            return bank
 
         xw = sb("xw", [P, T], U32)
         xs = sb("xs", [P, T], U8)
         w1w_raw = sb("w1w_raw", [P, H], U32)
         w1s_raw = sb("w1s_raw", [P, H], U8)
         tab_win = [sb("tab_win%d" % t, [P, J + SPARE], F32) for t in range(PACK)]
-        y_win = [sb("y_win%d" % t, [P, S + SPARE], F32) for t in range(PACK)]
-        a_win = [sb("a_win%d" % t, [P, S + SPARE], F32) for t in range(PACK)]
+        y_win = [sb("y_win%d" % t, [P, 2 * S], F32) for t in range(PACK)]
+        a_win = [sb("a_win%d" % t, [P, 2 * S], F32) for t in range(PACK)]
         b_win = [sb("b_win%d" % t, [P, 2 * S], F32) for t in range(PACK)]
         wb_raw = sb("wb_raw", [P, PACK, S], F32)
         gs_sb = sb("gs_sb", [P, PACK], F32)
@@ -66,108 +92,115 @@ def tile_picked_cdswpxbkind_none_po_kernel(
         z_codes = sb("z_codes", [P, S], U32)
         z_scale = sb("z_scale", [P, S], U8)
 
+        nc.vector.memset(w1s_raw[:].bitcast(I32), 0)
         nc.vector.memset(wb_scale[:].bitcast(I32), 0)
         nc.vector.memset(z_scale[:].bitcast(I32), 0)
         for t in range(PACK):
             nc.vector.memset(tab_win[t][:, J:], 0.0)
-        for t in range(PACK):
-            nc.vector.memset(y_win[t][:, S:], 0.0)
 
-        offs_sb = load_list("offs_sb", offs)
-        load_scale_rows_spread(nc.scalar, xs, x_scales)
-        cb_sb = load_list("cb_sb", cb)
-        cand_sb = load_list("cand_sb", cand)
-        nc.sync.dma_start(xw[:].bitcast(I32), x_words[0].rearrange("p n t -> p (n t)").bitcast(I32))
-        n1_sb = load_list("n1_sb", n1)
+        for q in range(4):
+            queue = nc.scalar if q < 2 else nc.sync
+            rows = x_scales[0, 4 * q : 4 * q + 4, :].bitcast(I32)
+            queue.dma_start(xs[32 * q : 32 * q + 32, :].bitcast(I32), rows.partition_broadcast(8))
         tab_rows = tab.rearrange("(p t) j -> p t j", t=PACK)
+        offs_sb = load_list("offs_sb", offs)
+        cb_sb = load_list("cb_sb", cb)
+        load_words(w1w_raw, w1_words)
+        load_words(xw, x_words)
+        n1_sb = load_list("n1_sb", n1)
         nc.sync.dma_start(tab_win[0][:, :J], tab_rows[:, 0, :])
-        nc.sync.dma_start(w1w_raw[:].bitcast(I32), w1_words[0].rearrange("p n t -> p (n t)").bitcast(I32))
-        load_scale_rows_spread(nc.sync, w1s_raw, w1_scales)
-        nc.gpsimd.dma_start(gs_sb[:], gs.rearrange("(p t) o -> p (t o)", t=PACK))
-        nc.gpsimd.dma_start(tau_sb[:], tau.rearrange("(p t) o -> p (t o)", t=PACK))
+        for q in range(4):
+            rows = w1_scales[0, 4 * q : 4 * q + 4, :].bitcast(I32)
+            nc.sync.dma_start(w1s_raw[32 * q : 32 * q + 4, :].bitcast(I32), rows)
         nc.sync.dma_start(tab_win[1][:, :J], tab_rows[:, 1, :])
+        cand_sb = load_list("cand_sb", cand)
         n2_sb = load_list("n2_sb", n2)
         nc.sync.dma_start(wb_raw[:], wb.rearrange("(p t) j -> p t j", t=PACK))
         for t in range(2, PACK):
             nc.sync.dma_start(tab_win[t][:, :J], tab_rows[:, t, :])
+        nc.sync.dma_start(gs_sb[:], gs.rearrange("(p t) o -> p (t o)", t=PACK))
+        nc.sync.dma_start(tau_sb[:], tau.rearrange("(p t) o -> p (t o)", t=PACK))
         n3_sb = load_list("n3_sb", n3)
         n4_sb = load_list("n4_sb", n4)
 
         xo_w = sb("xo_w", [P, S], U32)
         xo_s = sb("xo_s", [P, S], U8)
-        cb_w = sb("cb_w", [P, C], U32)
         cb_s = sb("cb_s", [P, C], U8)
         cd_w = sb("cd_w", [P, C], U32)
         cd_s = sb("cd_s", [P, C], U8)
+        w1_w = sb("w1_w", [P, H], U32)
+        w1_s = sb("w1_s", [P, H], U8)
+        wb_il = sb("wb_il", [P, S, PACK], BF16)
+
         nc.vector.tensor_copy(xo_s[:], xs[:].indirect(offs_sb[:]))
         nc.vector.tensor_copy(dealt(cb_s), xs[:].indirect(cb_sb[:]))
-        nc.vector.tensor_copy(dealt(cd_s), xs[:].indirect(cand_sb[:]))
         nc.vector.tensor_copy(xo_w[:], xw[:].indirect(offs_sb[:]))
-        w1_s = sb("w1_s", [P, H], U8)
-        nc.vector.tensor_copy(
-            w1_s[:].rearrange("p (t m) -> p t m", t=PACK), w1s_raw[:].rearrange("p (m t) -> p t m", t=PACK)
-        )
+        deal(nc.scalar.copy, w1_w, w1w_raw)
+        deal(nc.vector.tensor_copy, w1_s, w1s_raw)
+        y_ps = [product("ya%d" % t, w1_w, w1_s, xo_w, xo_s, t) for t in range(PACK)]
+        cb_w = sb("cb_w", [P, C], U32, tag="w1s_raw")
         nc.vector.tensor_copy(dealt(cb_w), xw[:].indirect(cb_sb[:]))
+        nc.vector.tensor_copy(dealt(cd_s), xs[:].indirect(cand_sb[:]))
         nc.vector.tensor_copy(dealt(cd_w), xw[:].indirect(cand_sb[:]))
 
-        w1_w = sb("w1_w", [P, H], U32)
-        tab_g = [sb("tab_g%d" % t, [P, S], F32) for t in range(PACK)]
-        nc.scalar.activation(tab_g[0][:], tab_win[0][:].indirect(n1_sb[:]), ACT.Copy)
-        nc.scalar.copy(
-            w1_w[:].rearrange("p (t m) -> p t m", t=PACK), w1w_raw[:].rearrange("p (m t) -> p t m", t=PACK)
-        )
-
-        def product(tag, lhs_w, lhs_s, rhs_w, rhs_s, t):
-            bank = psum.tile([P, S], F32, name=tag, tag=tag)
-            cols = slice(P * t, P * (t + 1))
-            nc.tensor.matmul_mx(
-                out=bank[:],
-                lhsT=lhs_w[:, cols].bitcast(FP8X4),
-                lhsT_scale=lhs_s[:, cols],
-                rhs=rhs_w[:].bitcast(FP8X4),
-                rhs_scale=rhs_s[:],
-                start=True,
-                stop=True,
-            )
-            return bank
-
-        y_ps = [product("ya%d" % t, w1_w, w1_s, xo_w, xo_s, t) for t in range(PACK)]
-
-        wb_il = sb("wb_il", [P, S, PACK], BF16)
-        interleave(nc.scalar.copy, wb_il, wb_raw)
-        for t in range(PACK):
-            nc.vector.memset(b_win[t][:, S:], 0.0)
-            nc.vector.memset(a_win[t][:, S:], 0.0)
-
+        tab_g = [y_win[t][:, S:] for t in range(PACK)]
         y_g = [sb("y_g%d" % t, [P, S], F32) for t in range(PACK)]
-        u = [sb("u%d" % t, [P, S], F32) for t in range(PACK)]
-        big = [sb("big%d" % t, [P, S], F32) for t in range(PACK)]
+        u = [a_win[t][:, S:] for t in range(PACK)]
+        big = [b_win[t][:, S:] for t in range(PACK)]
         z_pl = sb("z_pl", [P, PACK, S], BF16)
-        top = sb("top", [P, PACK], F32)
+        top = []
         bias = sb("bias", [P, PACK], F32)
-        ea = [sb("ea%d" % t, [P, S], F32) for t in range(PACK)]
-        b_ps = []
 
-        def z_scalar(t):
+        def z_gathers(t):
+            nc.scalar.activation(tab_g[t], tab_win[t][:].indirect(n1_sb[:]), ACT.Copy)
             nc.scalar.copy(y_win[t][:, :S], y_ps[t][:])
             nc.scalar.activation(y_g[t][:], y_win[t][:].indirect(n2_sb[:]), ACT.Copy)
-            if t + 1 < PACK:
-                nc.scalar.activation(tab_g[t + 1][:], tab_win[t + 1][:].indirect(n1_sb[:]), ACT.Copy)
 
-        def z_vector(t):
-            nc.vector.tensor_tensor(u[t][:], y_ps[t][:], tab_g[t][:], ALU.add)
-            nc.vector.tensor_tensor(big[t][:], u[t][:], y_g[t][:], ALU.max)
-            nc.vector.tensor_scalar(z_pl[:, t, :], big[t][:], gs_sb[:, t : t + 1], None, ALU.mult)
+        def z_add(t):
+            nc.vector.tensor_tensor(u[t], y_ps[t][:], tab_g[t], ALU.add)
 
-        def b_vector(t):
-            nc.vector.tensor_scalar(
-                b_win[t][:, :S], b_ps[t][:], 1.0, None, ALU.mult, ALU.max, accum_out=top[:, t : t + 1]
-            )
-            nc.vector.tensor_scalar(
-                bias[:, t : t + 1], top[:, t : t + 1], tau_sb[:, t : t + 1], -1.0, ALU.mult, ALU.mult
-            )
+        def z_max(t):
+            nc.vector.tensor_tensor(big[t], u[t], y_g[t][:], ALU.max)
 
-        def ea_scalar(t):
+        def z_gain(t, cols=WHOLE):
+            engine = nc.gpsimd if t in GAIN_ON_GPSIMD else nc.vector
+            engine.tensor_scalar(z_pl[:, t, cols], big[t][:, cols], gs_sb[:, t : t + 1], 0.0, ALU.mult, ALU.add)
+
+        def b_copy(t, top_tag=None):
+            top.append(sb("top%d" % t, [P, 1], F32, tag=top_tag))
+            nc.vector.tensor_scalar(b_win[t][:, :S], b_ps[t][:], 1.0, None, ALU.mult, ALU.max, accum_out=top[t][:])
+
+        def b_bias(t):
+            nc.gpsimd.tensor_scalar(bias[:, t : t + 1], top[t][:], tau_sb[:, t : t + 1], -1.0, ALU.mult, ALU.mult)
+
+        for t in range(PACK):
+            z_gathers(t)
+        z_add(0)
+        interleave(nc.vector.tensor_copy, wb_il[:], wb_raw[:])
+        z_max(0)
+        quantize(wb_codes[:], wb_scale[:], wb_il[:])
+        b_ps = [product("b%d" % t, cb_w, cb_s, wb_codes, wb_scale, t) for t in range(PACK)]
+        z_gain(0)
+        for t in range(1, PACK):
+            z_add(t)
+            b_copy(t - 1)
+            z_max(t)
+            for cols in HALVES if t == LAST else (WHOLE,):
+                z_gain(t, cols)
+            b_bias(t - 1)
+        z_il = sb("z_il", [P, S, PACK], BF16)
+        for cols in HALVES:
+            interleave(nc.vector.tensor_copy, z_il[:, cols, :], z_pl[:, :, cols])
+        for cols in HALVES:
+            quantize(z_codes[:, cols], z_scale[:, cols], z_il[:, cols, :])
+        b_copy(LAST, top_tag="z_il")
+        b_bias(LAST)
+
+        ea_tags = ("y_win3", "b_win0", "b_win1", "a_win2")
+        ea = []
+
+        def ea_gather(t):
+            ea.append(sb("ea%d" % t, [P, S], F32, tag=ea_tags[t]))
             nc.scalar.activation(
                 ea[t][:],
                 b_win[t][:].indirect(n3_sb[:]),
@@ -176,57 +209,74 @@ def tile_picked_cdswpxbkind_none_po_kernel(
                 scale=tau_sb[:, t : t + 1],
             )
 
-        z_scalar(0)
-        z_vector(0)
-        nc.vector.quantize_mx(
-            out=wb_codes[:].bitcast(FP8X4), scales=wb_scale[:], in_=wb_il[:].rearrange("p c t -> p (c t)")
-        )
-        for t in range(PACK):
-            b_ps.append(product("b%d" % t, cb_w, cb_s, wb_codes, wb_scale, t))
-        z_scalar(1)
-        z_vector(1)
-        b_vector(0)
-        z_scalar(2)
-        b_vector(1)
-        z_vector(2)
-        z_scalar(3)
-        b_vector(2)
-        z_vector(3)
-        z_il = sb("z_il", [P, S, PACK], BF16)
-        interleave(nc.vector.tensor_copy, z_il, z_pl)
-        nc.vector.quantize_mx(
-            out=z_codes[:].bitcast(FP8X4), scales=z_scale[:], in_=z_il[:].rearrange("p c t -> p (c t)")
-        )
-        b_vector(3)
-        for t in range(PACK - 1):
-            ea_scalar(t)
+        for t in range(LAST):
+            ea_gather(t)
 
-        a_ps = [product("ya%d" % t, cd_w, cd_s, z_codes, z_scale, t) for t in range(PACK)]
+        a_ps = [
+            product("ya%d" % t, cd_w, cd_s, z_codes, z_scale, t, HALVES if t == 0 else (WHOLE,)) for t in range(PACK)
+        ]
         a_g = [sb("a_g%d" % t, [P, S], F32) for t in range(PACK)]
         diff = [sb("diff%d" % t, [P, S], F32) for t in range(PACK)]
         prod = [sb("prod%d" % t, [P, S], F32) for t in range(PACK)]
         res = sb("res", [P, PACK, S], F32)
-        out_rows = out_0.rearrange("(p t) j -> p t j", t=PACK)
-        nc.vector.tensor_scalar(a_win[1][:, :S], a_ps[1][:], -0.125, None, ALU.mult)
-        for t in range(PACK):
-            if t != 1:
-                nc.scalar.activation(a_win[t][:, :S], a_ps[t][:], ACT.Copy, scale=-0.125)
-            nc.scalar.activation(a_g[t][:], a_win[t][:].indirect(n4_sb[:]), ACT.Copy)
-            nc.vector.scalar_tensor_tensor(diff[t][:], a_ps[t][:], 0.125, a_g[t][:], ALU.mult, ALU.add)
-            if t == PACK - 2:
-                ea_scalar(PACK - 1)
-            nc.vector.tensor_tensor(prod[t][:], diff[t][:], ea[t][:], ALU.mult)
-            nc.vector.scalar_tensor_tensor(res[:, t, :], b_ps[t][:], -0.5, prod[t][:], ALU.mult, ALU.add)
-            nc.sync.dma_start(out_rows[:, t, :], res[:, t, :])
-
         o_il = sb("o_il", [P, S, PACK], BF16)
         o_codes = sb("o_codes", [P, S], U32)
         o_scale = sb("o_scale", [P, S], U8)
-        interleave(nc.vector.tensor_copy, o_il, res)
-        nc.vector.quantize_mx(
-            out=o_codes[:].bitcast(FP8X4), scales=o_scale[:], in_=o_il[:].rearrange("p c t -> p (c t)")
-        )
-        nc.sync.dma_start(out_1[0].rearrange("p n t -> p (n t)").bitcast(I32), o_codes[:].bitcast(I32))
+        out_rows = out_0.rearrange("(p t) j -> p t j", t=PACK)
+        out_words = out_1[0].rearrange("p n t -> p (n t)").bitcast(I32)
+        twice_a = 2.0 * 0.0625
+
+        def a_copy(t):
+            nc.vector.tensor_scalar(a_win[t][:, :S], a_ps[t][:], -twice_a, None, ALU.mult)
+
+        def a_diff(t, cols=WHOLE):
+            places = n4_sb[:, cols.start // LIST_ROWS : cols.stop // LIST_ROWS]
+            nc.scalar.activation(a_g[t][:, cols], a_win[t][:].indirect(places), ACT.Copy)
+            nc.vector.scalar_tensor_tensor(
+                diff[t][:, cols], a_ps[t][:, cols], twice_a, a_g[t][:, cols], ALU.mult, ALU.add
+            )
+
+        def a_prod(t, cols=WHOLE):
+            engine = nc.gpsimd if t in PRODUCT_ON_GPSIMD else nc.vector
+            engine.tensor_tensor(prod[t][:, cols], diff[t][:, cols], ea[t][:, cols], ALU.mult)
+
+        def a_res(t, cols=WHOLE):
+            nc.vector.scalar_tensor_tensor(res[:, t, cols], b_ps[t][:, cols], -0.5, prod[t][:, cols], ALU.mult, ALU.add)
+
+        def store_res(t):
+            nc.sync.dma_start(out_rows[:, t, :], res[:, t, :])
+
+        def o_interleave(cols):
+            interleave(nc.vector.tensor_copy, o_il[:, cols, 2:4], res[:, 2:4, cols])
+
+        def o_quantize(cols):
+            quantize(o_codes[:, cols], o_scale[:, cols], o_il[:, cols, :])
+            nc.sync.dma_start(out_words[:, cols], o_codes[:, cols].bitcast(I32))
+
+        for t in range(PACK):
+            a_copy(t)
+        for t in range(LAST):
+            a_diff(t)
+            a_prod(t)
+            if t > 0:
+                a_res(t - 1)
+                store_res(t - 1)
+        ea_gather(LAST)
+        a_res(LAST - 1)
+        store_res(LAST - 1)
+
+        a_diff(LAST, FIRST_HALF)
+        a_prod(LAST, FIRST_HALF)
+        a_diff(LAST, SECOND_HALF)
+        interleave(nc.scalar.copy, o_il[:, :, 0:2], res[:, 0:2, :])
+        a_res(LAST, FIRST_HALF)
+        a_prod(LAST, SECOND_HALF)
+        o_interleave(FIRST_HALF)
+        a_res(LAST, SECOND_HALF)
+        store_res(LAST)
+        o_quantize(FIRST_HALF)
+        o_interleave(SECOND_HALF)
+        o_quantize(SECOND_HALF)
         for q in range(4):
             queue = nc.scalar if q % 2 == 0 else nc.sync
             queue.dma_start(out_2[0, 4 * q : 4 * q + 4, :].bitcast(I32), o_scale[32 * q : 32 * q + 4, :].bitcast(I32))

@@ -23,7 +23,7 @@ SPARE = 16
 WHOLE = slice(0, S)
 FIRST_HALF, SECOND_HALF = slice(0, S // 2), slice(S // 2, S)
 HALVES = (FIRST_HALF, SECOND_HALF)
-GAIN_ON_GPSIMD = (0, 1, 2)
+GAIN_ON_GPSIMD = (1, 2)
 PRODUCT_ON_GPSIMD = (0, 1)
 
 

from contextlib import ExitStack

import concourse.mybir as mybir

K, T, S, H, J, C = 512, 2048, 512, 512, 512, 512
FLOPS = 2 * K * C * S + 2 * K * H * S + 2 * H * C * S

F32 = mybir.dt.float32
BF16 = mybir.dt.bfloat16
I32 = mybir.dt.int32
U32 = mybir.dt.uint32
U16 = mybir.dt.uint16
U8 = mybir.dt.uint8
FP8X4 = mybir.dt.float8_e4m3fn_x4
ALU = mybir.AluOpType
ACT = mybir.ActivationFunctionType

P = 128
PACK = 4
LAST = PACK - 1
LIST_ROWS = 16
SPARE = 16
WHOLE = slice(0, S)
FIRST_HALF, SECOND_HALF = slice(0, S // 2), slice(S // 2, S)
HALVES = (FIRST_HALF, SECOND_HALF)
GAIN_ON_GPSIMD = (1, 2)
PRODUCT_ON_GPSIMD = (0, 1)


def tile_picked_cdswpxbkind_none_po_kernel(
    tc, x_words, x_scales, w1_words, w1_scales, tab, gs, wb, tau, offs, n1, n2, cand, cb, n3, n4, out_0, out_1, out_2
):
    nc = tc.nc
    with ExitStack() as ctx:
        keep = ctx.enter_context(tc.tile_pool(name="keep", bufs=1))
        psum = ctx.enter_context(tc.psum_pool(name="psum", bufs=1))

        def sb(name, shape, dtype, tag=None):
            return keep.tile(shape, dtype, name=name, tag=tag or name, align_bytes=64)

        def load_list(name, src):
            tile = sb(name, [P, S // LIST_ROWS], U16)
            nc.sync.dma_start(tile[:], src)
            return tile

        def load_words(tile, src):
            nc.sync.dma_start(tile[:].bitcast(I32), src[0].rearrange("p n t -> p (n t)").bitcast(I32))

        def dealt(tile):
            return tile[:].rearrange("p (t m) -> p m t", t=PACK)

        def deal(copy, dst, src):
            copy(dealt(dst), src[:].rearrange("p (m t) -> p m t", t=PACK))

        def interleave(copy, dst, src):
            copy(
                dst.rearrange("p (c i) t -> p c t i", i=4),
                src.rearrange("p t (c i) -> p c t i", i=4),
            )

        def quantize(codes, scale, src):
            nc.vector.quantize_mx(out=codes.bitcast(FP8X4), scales=scale, in_=src.rearrange("p c t -> p (c t)"))

        def product(tag, lhs_w, lhs_s, rhs_w, rhs_s, t, parts=(WHOLE,)):
            bank = psum.tile([P, S], F32, name=tag, tag=tag)
            rows = slice(P * t, P * (t + 1))
            for cols in parts:
                nc.tensor.matmul_mx(
                    out=bank[:, cols],
                    lhsT=lhs_w[:, rows].bitcast(FP8X4),
                    lhsT_scale=lhs_s[:, rows],
                    rhs=rhs_w[:, cols].bitcast(FP8X4),
                    rhs_scale=rhs_s[:, cols],
                    start=True,
                    stop=True,
                )
            return bank

        xw = sb("xw", [P, T], U32)
        xs = sb("xs", [P, T], U8)
        w1w_raw = sb("w1w_raw", [P, H], U32)
        w1s_raw = sb("w1s_raw", [P, H], U8)
        tab_win = [sb("tab_win%d" % t, [P, J + SPARE], F32) for t in range(PACK)]
        y_win = [sb("y_win%d" % t, [P, 2 * S], F32) for t in range(PACK)]
        a_win = [sb("a_win%d" % t, [P, 2 * S], F32) for t in range(PACK)]
        b_win = [sb("b_win%d" % t, [P, 2 * S], F32) for t in range(PACK)]
        wb_raw = sb("wb_raw", [P, PACK, S], F32)
        gs_sb = sb("gs_sb", [P, PACK], F32)
        tau_sb = sb("tau_sb", [P, PACK], F32)
        wb_codes = sb("wb_codes", [P, S], U32)
        wb_scale = sb("wb_scale", [P, S], U8)
        z_codes = sb("z_codes", [P, S], U32)
        z_scale = sb("z_scale", [P, S], U8)

        nc.vector.memset(w1s_raw[:].bitcast(I32), 0)
        nc.vector.memset(wb_scale[:].bitcast(I32), 0)
        nc.vector.memset(z_scale[:].bitcast(I32), 0)
        for t in range(PACK):
            nc.vector.memset(tab_win[t][:, J:], 0.0)

        for q in range(4):
            queue = nc.scalar if q < 2 else nc.sync
            rows = x_scales[0, 4 * q : 4 * q + 4, :].bitcast(I32)
            queue.dma_start(xs[32 * q : 32 * q + 32, :].bitcast(I32), rows.partition_broadcast(8))
        tab_rows = tab.rearrange("(p t) j -> p t j", t=PACK)
        offs_sb = load_list("offs_sb", offs)
        cb_sb = load_list("cb_sb", cb)
        load_words(w1w_raw, w1_words)
        load_words(xw, x_words)
        n1_sb = load_list("n1_sb", n1)
        nc.sync.dma_start(tab_win[0][:, :J], tab_rows[:, 0, :])
        for q in range(4):
            rows = w1_scales[0, 4 * q : 4 * q + 4, :].bitcast(I32)
            nc.sync.dma_start(w1s_raw[32 * q : 32 * q + 4, :].bitcast(I32), rows)
        nc.sync.dma_start(tab_win[1][:, :J], tab_rows[:, 1, :])
        cand_sb = load_list("cand_sb", cand)
        n2_sb = load_list("n2_sb", n2)
        nc.sync.dma_start(wb_raw[:], wb.rearrange("(p t) j -> p t j", t=PACK))
        for t in range(2, PACK):
            nc.sync.dma_start(tab_win[t][:, :J], tab_rows[:, t, :])
        nc.sync.dma_start(gs_sb[:], gs.rearrange("(p t) o -> p (t o)", t=PACK))
        nc.sync.dma_start(tau_sb[:], tau.rearrange("(p t) o -> p (t o)", t=PACK))
        n3_sb = load_list("n3_sb", n3)
        n4_sb = load_list("n4_sb", n4)

        xo_w = sb("xo_w", [P, S], U32)
        xo_s = sb("xo_s", [P, S], U8)
        cb_s = sb("cb_s", [P, C], U8)
        cd_w = sb("cd_w", [P, C], U32)
        cd_s = sb("cd_s", [P, C], U8)
        w1_w = sb("w1_w", [P, H], U32)
        w1_s = sb("w1_s", [P, H], U8)
        wb_il = sb("wb_il", [P, S, PACK], BF16)

        nc.vector.tensor_copy(xo_s[:], xs[:].indirect(offs_sb[:]))
        nc.vector.tensor_copy(dealt(cb_s), xs[:].indirect(cb_sb[:]))
        nc.vector.tensor_copy(xo_w[:], xw[:].indirect(offs_sb[:]))
        deal(nc.scalar.copy, w1_w, w1w_raw)
        deal(nc.vector.tensor_copy, w1_s, w1s_raw)
        y_ps = [product("ya%d" % t, w1_w, w1_s, xo_w, xo_s, t) for t in range(PACK)]
        cb_w = sb("cb_w", [P, C], U32, tag="w1s_raw")
        nc.vector.tensor_copy(dealt(cb_w), xw[:].indirect(cb_sb[:]))
        nc.vector.tensor_copy(dealt(cd_s), xs[:].indirect(cand_sb[:]))
        nc.vector.tensor_copy(dealt(cd_w), xw[:].indirect(cand_sb[:]))

        tab_g = [y_win[t][:, S:] for t in range(PACK)]
        y_g = [sb("y_g%d" % t, [P, S], F32) for t in range(PACK)]
        u = [a_win[t][:, S:] for t in range(PACK)]
        big = [b_win[t][:, S:] for t in range(PACK)]
        z_pl = sb("z_pl", [P, PACK, S], BF16)
        top = []
        bias = sb("bias", [P, PACK], F32)

        def z_gathers(t):
            nc.scalar.activation(tab_g[t], tab_win[t][:].indirect(n1_sb[:]), ACT.Copy)
            nc.scalar.copy(y_win[t][:, :S], y_ps[t][:])
            nc.scalar.activation(y_g[t][:], y_win[t][:].indirect(n2_sb[:]), ACT.Copy)

        def z_add(t):
            nc.vector.tensor_tensor(u[t], y_ps[t][:], tab_g[t], ALU.add)

        def z_max(t):
            nc.vector.tensor_tensor(big[t], u[t], y_g[t][:], ALU.max)

        def z_gain(t, cols=WHOLE):
            engine = nc.gpsimd if t in GAIN_ON_GPSIMD else nc.vector
            engine.tensor_scalar(z_pl[:, t, cols], big[t][:, cols], gs_sb[:, t : t + 1], 0.0, ALU.mult, ALU.add)

        def b_copy(t, top_tag=None):
            top.append(sb("top%d" % t, [P, 1], F32, tag=top_tag))
            nc.vector.tensor_scalar(b_win[t][:, :S], b_ps[t][:], 1.0, None, ALU.mult, ALU.max, accum_out=top[t][:])

        def b_bias(t):
            nc.gpsimd.tensor_scalar(bias[:, t : t + 1], top[t][:], tau_sb[:, t : t + 1], -1.0, ALU.mult, ALU.mult)

        for t in range(PACK):
            z_gathers(t)
        z_add(0)
        interleave(nc.vector.tensor_copy, wb_il[:], wb_raw[:])
        z_max(0)
        quantize(wb_codes[:], wb_scale[:], wb_il[:])
        b_ps = [product("b%d" % t, cb_w, cb_s, wb_codes, wb_scale, t) for t in range(PACK)]
        z_gain(0)
        for t in range(1, PACK):
            z_add(t)
            b_copy(t - 1)
            z_max(t)
            for cols in HALVES if t == LAST else (WHOLE,):
                z_gain(t, cols)
            b_bias(t - 1)
        z_il = sb("z_il", [P, S, PACK], BF16)
        for cols in HALVES:
            interleave(nc.vector.tensor_copy, z_il[:, cols, :], z_pl[:, :, cols])
        for cols in HALVES:
            quantize(z_codes[:, cols], z_scale[:, cols], z_il[:, cols, :])
        b_copy(LAST, top_tag="z_il")
        b_bias(LAST)

        ea_tags = ("y_win3", "b_win0", "b_win1", "a_win2")
        ea = []

        def ea_gather(t):
            ea.append(sb("ea%d" % t, [P, S], F32, tag=ea_tags[t]))
            nc.scalar.activation(
                ea[t][:],
                b_win[t][:].indirect(n3_sb[:]),
                ACT.Exp,
                bias=bias[:, t : t + 1],
                scale=tau_sb[:, t : t + 1],
            )

        for t in range(LAST):
            ea_gather(t)

        a_ps = [
            product("ya%d" % t, cd_w, cd_s, z_codes, z_scale, t, HALVES if t == 0 else (WHOLE,)) for t in range(PACK)
        ]
        a_g = [sb("a_g%d" % t, [P, S], F32) for t in range(PACK)]
        diff = [sb("diff%d" % t, [P, S], F32) for t in range(PACK)]
        prod = [sb("prod%d" % t, [P, S], F32) for t in range(PACK)]
        res = sb("res", [P, PACK, S], F32)
        o_il = sb("o_il", [P, S, PACK], BF16)
        o_codes = sb("o_codes", [P, S], U32)
        o_scale = sb("o_scale", [P, S], U8)
        out_rows = out_0.rearrange("(p t) j -> p t j", t=PACK)
        out_words = out_1[0].rearrange("p n t -> p (n t)").bitcast(I32)
        twice_a = 2.0 * 0.0625

        def a_copy(t):
            nc.vector.tensor_scalar(a_win[t][:, :S], a_ps[t][:], -twice_a, None, ALU.mult)

        def a_diff(t, cols=WHOLE):
            places = n4_sb[:, cols.start // LIST_ROWS : cols.stop // LIST_ROWS]
            nc.scalar.activation(a_g[t][:, cols], a_win[t][:].indirect(places), ACT.Copy)
            nc.vector.scalar_tensor_tensor(
                diff[t][:, cols], a_ps[t][:, cols], twice_a, a_g[t][:, cols], ALU.mult, ALU.add
            )

        def a_prod(t, cols=WHOLE):
            engine = nc.gpsimd if t in PRODUCT_ON_GPSIMD else nc.vector
            engine.tensor_tensor(prod[t][:, cols], diff[t][:, cols], ea[t][:, cols], ALU.mult)

        def a_res(t, cols=WHOLE):
            nc.vector.scalar_tensor_tensor(res[:, t, cols], b_ps[t][:, cols], -0.5, prod[t][:, cols], ALU.mult, ALU.add)

        def store_res(t):
            nc.sync.dma_start(out_rows[:, t, :], res[:, t, :])

        def o_interleave(cols):
            interleave(nc.vector.tensor_copy, o_il[:, cols, 2:4], res[:, 2:4, cols])

        def o_quantize(cols):
            quantize(o_codes[:, cols], o_scale[:, cols], o_il[:, cols, :])
            nc.sync.dma_start(out_words[:, cols], o_codes[:, cols].bitcast(I32))

        for t in range(PACK):
            a_copy(t)
        for t in range(LAST):
            a_diff(t)
            a_prod(t)
            if t > 0:
                a_res(t - 1)
                store_res(t - 1)
        ea_gather(LAST)
        a_res(LAST - 1)
        store_res(LAST - 1)

        a_diff(LAST, FIRST_HALF)
        a_prod(LAST, FIRST_HALF)
        a_diff(LAST, SECOND_HALF)
        interleave(nc.scalar.copy, o_il[:, :, 0:2], res[:, 0:2, :])
        a_res(LAST, FIRST_HALF)
        a_prod(LAST, SECOND_HALF)
        o_interleave(FIRST_HALF)
        a_res(LAST, SECOND_HALF)
        store_res(LAST)
        o_quantize(FIRST_HALF)
        o_interleave(SECOND_HALF)
        o_quantize(SECOND_HALF)
        for q in range(4):
            queue = nc.scalar if q % 2 == 0 else nc.sync
            queue.dma_start(out_2[0, 4 * q : 4 * q + 4, :].bitcast(I32), o_scale[32 * q : 32 * q + 4, :].bitcast(I32))
